import numpy as np
CORES = [16,20,144,148]
N = 4
def setup_inputs(rng):
    return {"x": rng.standard_normal((N, 128, 8), dtype=np.float32)}
def reference(x):
    b = 8 // N
    blocks = x.reshape(N, 128, N, b)
    return {"y": np.ascontiguousarray(blocks.transpose(2, 1, 0, 3)).reshape(N, 128, 8)}

@@ -1,0 +1,45 @@
+from concourse.bass import DstId, RemoteDMATransfer
+
+SCRATCH = {
+    "send": ("sbuf", [128, 8], "float32"),
+    "land": ("sbuf", [128, 8], "float32"),
+}
+SEMAPHORES = ["loaded", "own", "arrived", "stored"]
+
+ON_CHIP_MASK = 0xFF00
+OFF_CHIP_MASKS = (0x000F, 0x00F0)
+
+
+def rank_program(g, core, T, topo):
+    r = T.rank_of(core)
+    if r is None:
+        return
+    n = len(T.cores)
+    b = T.x.shape[1] // n
+
+    def blk(t, j):
+        return t[:, j * b:(j + 1) * b]
+
+    g.dma_start(T.send[:], T.x[:]).then_inc(T.sem.loaded, 16)
+    g.dma_start(blk(T.land, r), blk(T.x, r)).then_inc(T.sem.own, 16)
+
+    transfers = []
+    off = 0
+    for j, d in enumerate(T.cores):
+        if j == r:
+            continue
+        rid, pid = topo.addr(d, core)
+        if topo.mask(core, d) == 0xFFFF:
+            m = ON_CHIP_MASK
+        else:
+            m = OFF_CHIP_MASKS[off]
+            off += 1
+        transfers.append(RemoteDMATransfer(dst_ids=[DstId(rid=rid, pnc=pid)], dma_engine_mask=m,
+                                           remote_sem=T.sem.arrived, src=blk(T.send, j), dst=blk(T.land, r)))
+    g.wait_ge(T.sem.loaded, 16)
+    g.remote_dma_fused(transfers, local_sem=T.sem.arrived)
+
+    g.wait_ge(T.sem.arrived, 32)
+    g.wait_ge(T.sem.own, 16)
+    g.dma_start(T.y[:], T.land[:]).then_inc(T.sem.stored, 16)
+    g.wait_ge(T.sem.stored, 16)

@@ -23,23 +23,21 @@ def rank_program(g, core, T, topo):
     g.dma_start(T.send[:], T.x[:]).then_inc(T.sem.loaded, 16)
     g.dma_start(blk(T.land, r), blk(T.x, r)).then_inc(T.sem.own, 16)
 
+    far = [j for j, d in enumerate(T.cores) if j != r and topo.mask(core, d) != 0xFFFF]
+    near = [j for j, d in enumerate(T.cores) if j != r and topo.mask(core, d) == 0xFFFF]
+    far.sort(key=lambda j: topo.die(T.cores[j]) == topo.die(core))
     transfers = []
-    off = 0
-    for j, d in enumerate(T.cores):
-        if j == r:
-            continue
-        rid, pid = topo.addr(d, core)
-        if topo.mask(core, d) == 0xFFFF:
-            m = ON_CHIP_MASK
-        else:
-            m = OFF_CHIP_MASKS[off]
-            off += 1
+    for j, m in zip(far, OFF_CHIP_MASKS):
+        rid, pid = topo.addr(T.cores[j], core)
         transfers.append(RemoteDMATransfer(dst_ids=[DstId(rid=rid, pnc=pid)], dma_engine_mask=m,
                                            remote_sem=T.sem.arrived, src=blk(T.send, j), dst=blk(T.land, r)))
     g.wait_ge(T.sem.loaded, 16)
     g.remote_dma_fused(transfers, local_sem=T.sem.arrived)
+    for j in near:
+        rid, pid = topo.addr(T.cores[j], core)
+        g.remote_dma(blk(T.land, r), blk(T.send, j), T.sem.arrived, T.sem.arrived, pid, rid, ON_CHIP_MASK)
 
-    g.wait_ge(T.sem.arrived, 32)
     g.wait_ge(T.sem.own, 16)
+    g.wait_ge(T.sem.arrived, 32)
     g.dma_start(T.y[:], T.land[:]).then_inc(T.sem.stored, 16)
     g.wait_ge(T.sem.stored, 16)

from concourse.bass import DstId, RemoteDMATransfer

SCRATCH = {
    "send": ("sbuf", [128, 8], "float32"),
    "land": ("sbuf", [128, 8], "float32"),
}
SEMAPHORES = ["loaded", "own", "arrived", "stored"]

ON_CHIP_MASK = 0xFF00
OFF_CHIP_MASKS = (0x000F, 0x00F0)


def rank_program(g, core, T, topo):
    r = T.rank_of(core)
    if r is None:
        return
    n = len(T.cores)
    b = T.x.shape[1] // n

    def blk(t, j):
        return t[:, j * b:(j + 1) * b]

    g.dma_start(T.send[:], T.x[:]).then_inc(T.sem.loaded, 16)
    g.dma_start(blk(T.land, r), blk(T.x, r)).then_inc(T.sem.own, 16)

    far = [j for j, d in enumerate(T.cores) if j != r and topo.mask(core, d) != 0xFFFF]
    near = [j for j, d in enumerate(T.cores) if j != r and topo.mask(core, d) == 0xFFFF]
    far.sort(key=lambda j: topo.die(T.cores[j]) == topo.die(core))
    transfers = []
    for j, m in zip(far, OFF_CHIP_MASKS):
        rid, pid = topo.addr(T.cores[j], core)
        transfers.append(RemoteDMATransfer(dst_ids=[DstId(rid=rid, pnc=pid)], dma_engine_mask=m,
                                           remote_sem=T.sem.arrived, src=blk(T.send, j), dst=blk(T.land, r)))
    g.wait_ge(T.sem.loaded, 16)
    g.remote_dma_fused(transfers, local_sem=T.sem.arrived)
    for j in near:
        rid, pid = topo.addr(T.cores[j], core)
        g.remote_dma(blk(T.land, r), blk(T.send, j), T.sem.arrived, T.sem.arrived, pid, rid, ON_CHIP_MASK)

    g.wait_ge(T.sem.own, 16)
    g.wait_ge(T.sem.arrived, 32)
    g.dma_start(T.y[:], T.land[:]).then_inc(T.sem.stored, 16)
    g.wait_ge(T.sem.stored, 16)
